import numpy as np, ml_dtypes
CORES = [10,34,74,98]
N = 4
KB, QP = 2, 256
MEM = [0]
def setup_inputs(rng):
    return {"q": rng.standard_normal((N, 128, QP), dtype=np.float32).astype(ml_dtypes.bfloat16), "k": rng.standard_normal((N, 128, KB * 128), dtype=np.float32).astype(ml_dtypes.bfloat16), "v": rng.standard_normal((N, 128, KB * 128), dtype=np.float32).astype(ml_dtypes.bfloat16)}
def setup_inputs_big(rng):
    d = setup_inputs(rng)
    for k in ("q", "k", "v"): d[k] = (d[k].astype(np.float32) * 1024.0).astype(d[k].dtype)
    return d
def setup_inputs_small(rng):
    d = setup_inputs(rng)
    for k in ("q", "k", "v"): d[k] = (d[k].astype(np.float32) * (1 / 1024.0)).astype(d[k].dtype)
    return d
def setup_inputs_apart(rng):
    d = setup_inputs(rng)
    f = (10.0 ** rng.permutation(np.linspace(-1.5, 1.5, N))).astype(np.float32).reshape(N, 1, 1)
    for k in ("q", "k", "v"): d[k] = (d[k].astype(np.float32) * f).astype(d[k].dtype)
    return d
def reference(q, k, v):
    Q, K, V = q.astype(np.float64), k.astype(np.float64), v.astype(np.float64)
    y = np.zeros((N, 128, QP))
    for r in range(N):
        for j in MEM:
            for b in range(KB):
                S = np.maximum(K[j][:, 128 * b:128 * b + 128].T @ Q[r], 0.0)
                y[r] += V[j][:, 128 * b:128 * b + 128].T @ S
    return {"y": y.astype(ml_dtypes.bfloat16 if q.dtype != np.float64 else np.float64)}

@@ -1,0 +1,139 @@
+from concourse.bass import DstId, RemoteDMATransfer
+from concourse.mybir import AluOpType
+
+P = 128
+KB = 2
+QP = 256
+H = 2
+W = QP // H
+
+SCRATCH = {
+    "kv": ("sbuf", [P, 2 * KB * P], "bfloat16"),
+    "qs": ("sbuf", [P, QP], "bfloat16"),
+    "qb": ("sbuf", [P, QP], "bfloat16"),
+    "zero": ("sbuf", [P, W], "float32"),
+    "s0": ("sbuf", [P, KB * QP], "bfloat16"),
+    "s1": ("sbuf", [P, KB * QP], "bfloat16"),
+    "yo0": ("sbuf", [P, QP], "bfloat16"),
+    "yo1": ("sbuf", [P, QP], "bfloat16"),
+    "qd": ("dram", [P, QP], "bfloat16"),
+    "yd": ("dram", [P, QP], "bfloat16"),
+}
+for _b in range(KB):
+    for _h in range(H):
+        SCRATCH["ps%d%d" % (_b, _h)] = ("psum", [P, 512], "float32")
+for _h in range(H):
+    SCRATCH["po%d" % _h] = ("psum", [P, 512], "float32")
+
+SEMAPHORES = ["ld", "lq", "z", "akv", "skv", "aq", "sq", "ay", "sy", "st"]
+for _r in range(2):
+    SEMAPHORES.append("c%d" % _r)
+    for _h in range(H):
+        SEMAPHORES.append("o%d%d" % (_r, _h))
+        for _b in range(KB):
+            SEMAPHORES.append("m%d%d%d" % (_r, _b, _h))
+            SEMAPHORES.append("r%d%d%d" % (_r, _b, _h))
+
+
+def _engines(mask):
+    return bin(mask).count("1")
+
+
+def _attend(g, T, rnd, q, s, y, ready, banks_free):
+    sem, te, ve = T.sem, g.tensor, g.vector
+    for name, val in ready:
+        te.wait_ge(sem[name], val)
+    for h in range(H):
+        for b in range(KB):
+            te.matmul(T["ps%d%d" % (b, h)][:, 0:W], T.kv[:, P * b:P * (b + 1)], q[:, W * h:W * (h + 1)],
+                      start=True, stop=True).then_inc(sem["m%d%d%d" % (rnd, b, h)], 1)
+    for name, val in banks_free:
+        te.wait_ge(sem[name], val)
+    for h in range(H):
+        for b in range(KB):
+            j = KB * h + b
+            te.wait_ge(sem["r%d%d%d" % (rnd, b, h)], 1)
+            te.matmul(T["po%d" % h][:, 0:W], T.kv[:, P * (KB + b):P * (KB + b + 1)], s[:, W * j:W * (j + 1)],
+                      start=(b == 0), stop=(b == KB - 1)).then_inc(sem["o%d%d" % (rnd, h)], 1)
+    for h in range(H):
+        for b in range(KB):
+            j = KB * h + b
+            ve.wait_ge(sem["m%d%d%d" % (rnd, b, h)], 1)
+            ve.tensor_tensor(s[:, W * j:W * (j + 1)], T["ps%d%d" % (b, h)][:, 0:W], T.zero[:],
+                             AluOpType.max).then_inc(sem["r%d%d%d" % (rnd, b, h)], 1)
+    for h in range(H):
+        ve.wait_ge(sem["o%d%d" % (rnd, h)], KB)
+        ve.tensor_copy(y[:, W * h:W * (h + 1)], T["po%d" % h][:, 0:W]).then_inc(sem["c%d" % rnd], 1)
+
+
+def _roles(T, topo):
+    mem = T.cores[T.tables["MEM"][0]]
+    others = [c for c in T.cores if c != mem]
+    near = [c for c in others if topo.chip(c) == topo.chip(mem) or topo.same_plane(topo.chip(mem), topo.chip(c))]
+    far = [c for c in others if c not in near]
+    back = (far if len(far) >= len(near) else near)[-1]
+    fwd = [c for c in others if c != back]
+    for c in others:
+        if not (topo.may_write(mem, c) and topo.may_write(c, mem)):
+            raise ValueError("no direct write between cores %d and %d" % (mem, c))
+    return mem, fwd, back
+
+
+def rank_program(g, core, T, topo):
+    if T.rank_of(core) is None:
+        return
+    sem = T.sem
+    mem, fwd, back = _roles(T, topo)
+    KW = KB * P
+
+    if core == back:
+        m = topo.mask(core, mem)
+        rid, pid, _ = topo.addr(mem)
+        g.sync.dma_start(T.qd[:], T.q[:]).then_inc(sem.lq, 16)
+        g.wait_ge(sem.lq, 16)
+        g.remote_dma(T.qb[:], T.qd[:], remote_sem=sem.aq, local_sem=sem.sq, pid=pid, routing_id=rid,
+                     dma_engine_mask=m)
+        g.sync.wait_ge(sem.ay, _engines(topo.mask(mem, core)))
+        g.sync.dma_start(T.y[:], T.yd[:]).then_inc(sem.st, 16)
+        g.sync.wait_ge(sem.st, 16)
+        g.wait_ge(sem.sq, _engines(m))
+        return
+
+    g.vector.memset(T.zero[:], 0.0).then_inc(sem.z, 1)
+    g.vector.wait_ge(sem.z, 1)
+
+    if core != mem:
+        g.sync.dma_start(T.qs[:], T.q[:]).then_inc(sem.lq, 16)
+        _attend(g, T, 0, T.qs, T.s0, T.yo0, [("lq", 16), ("akv", _engines(topo.mask(mem, core)))], [])
+        g.sync.wait_ge(sem.c0, H)
+        g.sync.dma_start(T.y[:], T.yo0[:]).then_inc(sem.st, 16)
+        g.sync.wait_ge(sem.st, 16)
+        return
+
+    g.sync.dma_start(T.kv[:, 0:KW], T.k[:]).then_inc(sem.ld, 16)
+    g.scalar.dma_start(T.kv[:, KW:2 * KW], T.v[:]).then_inc(sem.ld, 16)
+    g.sync.dma_start(T.qs[:], T.q[:]).then_inc(sem.lq, 16)
+
+    mk = topo.mask(core, fwd[0])
+    for c in fwd:
+        mk &= topo.mask(core, c)
+    g.wait_ge(sem.ld, 32)
+    g.remote_dma_fused([RemoteDMATransfer(
+        dst_ids=[DstId(rid=topo.addr(c)[0], pnc=topo.addr(c)[1]) for c in fwd],
+        dma_engine_mask=mk, remote_sem=sem.akv, srcs=[T.kv[:]], dsts=[T.kv[:] for c in fwd], alu_op=0)],
+        local_sem=sem.skv)
+
+    _attend(g, T, 0, T.qs, T.s0, T.yo0, [("ld", 32), ("lq", 16)], [])
+    _attend(g, T, 1, T.qb, T.s1, T.yo1, [("aq", _engines(topo.mask(back, core)))], [("c0", H)])
+
+    mb = topo.mask(core, back)
+    rid, pid, _ = topo.addr(back)
+    g.wait_ge(sem.c1, H)
+    g.remote_dma(T.yd[:], T.yo1[:], remote_sem=sem.ay, local_sem=sem.sy, pid=pid, routing_id=rid,
+                 dma_engine_mask=mb)
+
+    g.sync.wait_ge(sem.c0, H)
+    g.sync.wait_ge(sem.skv, _engines(mk))
+    g.sync.dma_start(T.y[:], T.yo0[:]).then_inc(sem.st, 16)
+    g.sync.wait_ge(sem.st, 16)
+    g.wait_ge(sem.sy, _engines(mb))

@@ -25,7 +25,7 @@ for _b in range(KB):
 for _h in range(H):
     SCRATCH["po%d" % _h] = ("psum", [P, 512], "float32")
 
-SEMAPHORES = ["ld", "lq", "z", "akv", "skv", "aq", "sq", "ay", "sy", "st"]
+SEMAPHORES = ["lk", "lv", "lq", "z", "ak", "av", "skv", "aq", "sq", "ay", "sy", "st"]
 for _r in range(2):
     SEMAPHORES.append("c%d" % _r)
     for _h in range(H):
@@ -39,15 +39,15 @@ def _engines(mask):
     return bin(mask).count("1")
 
 
-def _attend(g, T, rnd, q, s, y, ready, banks_free):
+def _attend(g, T, rnd, q, s, y, ready_k, ready_v):
     sem, te, ve = T.sem, g.tensor, g.vector
-    for name, val in ready:
+    for name, val in ready_k:
         te.wait_ge(sem[name], val)
     for h in range(H):
         for b in range(KB):
             te.matmul(T["ps%d%d" % (b, h)][:, 0:W], T.kv[:, P * b:P * (b + 1)], q[:, W * h:W * (h + 1)],
                       start=True, stop=True).then_inc(sem["m%d%d%d" % (rnd, b, h)], 1)
-    for name, val in banks_free:
+    for name, val in ready_v:
         te.wait_ge(sem[name], val)
     for h in range(H):
         for b in range(KB):
@@ -66,12 +66,17 @@ def _attend(g, T, rnd, q, s, y, ready, banks_free):
         ve.tensor_copy(y[:, W * h:W * (h + 1)], T["po%d" % h][:, 0:W]).then_inc(sem["c%d" % rnd], 1)
 
 
+def _hops(topo, a, b):
+    ca, cb = topo.chip(a), topo.chip(b)
+    if ca == cb:
+        return 0
+    return 1 if (topo.mates(ca, cb) or topo.same_plane(ca, cb)) else 2
+
+
 def _roles(T, topo):
     mem = T.cores[T.tables["MEM"][0]]
     others = [c for c in T.cores if c != mem]
-    near = [c for c in others if topo.chip(c) == topo.chip(mem) or topo.same_plane(topo.chip(mem), topo.chip(c))]
-    far = [c for c in others if c not in near]
-    back = (far if len(far) >= len(near) else near)[-1]
+    back = min(others, key=lambda c: _hops(topo, mem, c))
     fwd = [c for c in others if c != back]
     for c in others:
         if not (topo.may_write(mem, c) and topo.may_write(c, mem)):
@@ -103,27 +108,29 @@ def rank_program(g, core, T, topo):
     g.vector.wait_ge(sem.z, 1)
 
     if core != mem:
+        n = _engines(topo.mask(mem, core))
         g.sync.dma_start(T.qs[:], T.q[:]).then_inc(sem.lq, 16)
-        _attend(g, T, 0, T.qs, T.s0, T.yo0, [("lq", 16), ("akv", _engines(topo.mask(mem, core)))], [])
+        _attend(g, T, 0, T.qs, T.s0, T.yo0, [("lq", 16), ("ak", n)], [("av", n)])
         g.sync.wait_ge(sem.c0, H)
         g.sync.dma_start(T.y[:], T.yo0[:]).then_inc(sem.st, 16)
         g.sync.wait_ge(sem.st, 16)
         return
 
-    g.sync.dma_start(T.kv[:, 0:KW], T.k[:]).then_inc(sem.ld, 16)
-    g.scalar.dma_start(T.kv[:, KW:2 * KW], T.v[:]).then_inc(sem.ld, 16)
+    g.sync.dma_start(T.kv[:, 0:KW], T.k[:]).then_inc(sem.lk, 16)
+    g.sync.dma_start(T.kv[:, KW:2 * KW], T.v[:]).then_inc(sem.lv, 16)
     g.sync.dma_start(T.qs[:], T.q[:]).then_inc(sem.lq, 16)
 
     mk = topo.mask(core, fwd[0])
     for c in fwd:
         mk &= topo.mask(core, c)
-    g.wait_ge(sem.ld, 32)
-    g.remote_dma_fused([RemoteDMATransfer(
-        dst_ids=[DstId(rid=topo.addr(c)[0], pnc=topo.addr(c)[1]) for c in fwd],
-        dma_engine_mask=mk, remote_sem=sem.akv, srcs=[T.kv[:]], dsts=[T.kv[:] for c in fwd], alu_op=0)],
-        local_sem=sem.skv)
+    ids = [DstId(rid=topo.addr(c)[0], pnc=topo.addr(c)[1]) for c in fwd]
+    for lo, loaded, arrived in ((0, sem.lk, sem.ak), (KW, sem.lv, sem.av)):
+        g.wait_ge(loaded, 16)
+        g.remote_dma_fused([RemoteDMATransfer(
+            dst_ids=ids, dma_engine_mask=mk, remote_sem=arrived, srcs=[T.kv[:, lo:lo + KW]],
+            dsts=[T.kv[:, lo:lo + KW] for c in fwd], alu_op=0)], local_sem=sem.skv)
 
-    _attend(g, T, 0, T.qs, T.s0, T.yo0, [("ld", 32), ("lq", 16)], [])
+    _attend(g, T, 0, T.qs, T.s0, T.yo0, [("lk", 16), ("lq", 16)], [("lv", 16)])
     _attend(g, T, 1, T.qb, T.s1, T.yo1, [("aq", _engines(topo.mask(back, core)))], [("c0", H)])
 
     mb = topo.mask(core, back)
@@ -133,7 +140,7 @@ def rank_program(g, core, T, topo):
                  dma_engine_mask=mb)
 
     g.sync.wait_ge(sem.c0, H)
-    g.sync.wait_ge(sem.skv, _engines(mk))
+    g.sync.wait_ge(sem.skv, 2 * _engines(mk))
     g.sync.dma_start(T.y[:], T.yo0[:]).then_inc(sem.st, 16)
     g.sync.wait_ge(sem.st, 16)
     g.wait_ge(sem.sy, _engines(mb))

from concourse.bass import DstId, RemoteDMATransfer
from concourse.mybir import AluOpType

P = 128
KB = 2
QP = 256
H = 2
W = QP // H

SCRATCH = {
    "kv": ("sbuf", [P, 2 * KB * P], "bfloat16"),
    "qs": ("sbuf", [P, QP], "bfloat16"),
    "qb": ("sbuf", [P, QP], "bfloat16"),
    "zero": ("sbuf", [P, W], "float32"),
    "s0": ("sbuf", [P, KB * QP], "bfloat16"),
    "s1": ("sbuf", [P, KB * QP], "bfloat16"),
    "yo0": ("sbuf", [P, QP], "bfloat16"),
    "yo1": ("sbuf", [P, QP], "bfloat16"),
    "qd": ("dram", [P, QP], "bfloat16"),
    "yd": ("dram", [P, QP], "bfloat16"),
}
for _b in range(KB):
    for _h in range(H):
        SCRATCH["ps%d%d" % (_b, _h)] = ("psum", [P, 512], "float32")
for _h in range(H):
    SCRATCH["po%d" % _h] = ("psum", [P, 512], "float32")

SEMAPHORES = ["lk", "lv", "lq", "z", "ak", "av", "skv", "aq", "sq", "ay", "sy", "st"]
for _r in range(2):
    SEMAPHORES.append("c%d" % _r)
    for _h in range(H):
        SEMAPHORES.append("o%d%d" % (_r, _h))
        for _b in range(KB):
            SEMAPHORES.append("m%d%d%d" % (_r, _b, _h))
            SEMAPHORES.append("r%d%d%d" % (_r, _b, _h))


def _engines(mask):
    return bin(mask).count("1")


def _attend(g, T, rnd, q, s, y, ready_k, ready_v):
    sem, te, ve = T.sem, g.tensor, g.vector
    for name, val in ready_k:
        te.wait_ge(sem[name], val)
    for h in range(H):
        for b in range(KB):
            te.matmul(T["ps%d%d" % (b, h)][:, 0:W], T.kv[:, P * b:P * (b + 1)], q[:, W * h:W * (h + 1)],
                      start=True, stop=True).then_inc(sem["m%d%d%d" % (rnd, b, h)], 1)
    for name, val in ready_v:
        te.wait_ge(sem[name], val)
    for h in range(H):
        for b in range(KB):
            j = KB * h + b
            te.wait_ge(sem["r%d%d%d" % (rnd, b, h)], 1)
            te.matmul(T["po%d" % h][:, 0:W], T.kv[:, P * (KB + b):P * (KB + b + 1)], s[:, W * j:W * (j + 1)],
                      start=(b == 0), stop=(b == KB - 1)).then_inc(sem["o%d%d" % (rnd, h)], 1)
    for h in range(H):
        for b in range(KB):
            j = KB * h + b
            ve.wait_ge(sem["m%d%d%d" % (rnd, b, h)], 1)
            ve.tensor_tensor(s[:, W * j:W * (j + 1)], T["ps%d%d" % (b, h)][:, 0:W], T.zero[:],
                             AluOpType.max).then_inc(sem["r%d%d%d" % (rnd, b, h)], 1)
    for h in range(H):
        ve.wait_ge(sem["o%d%d" % (rnd, h)], KB)
        ve.tensor_copy(y[:, W * h:W * (h + 1)], T["po%d" % h][:, 0:W]).then_inc(sem["c%d" % rnd], 1)


def _hops(topo, a, b):
    ca, cb = topo.chip(a), topo.chip(b)
    if ca == cb:
        return 0
    return 1 if (topo.mates(ca, cb) or topo.same_plane(ca, cb)) else 2


def _roles(T, topo):
    mem = T.cores[T.tables["MEM"][0]]
    others = [c for c in T.cores if c != mem]
    back = min(others, key=lambda c: _hops(topo, mem, c))
    fwd = [c for c in others if c != back]
    for c in others:
        if not (topo.may_write(mem, c) and topo.may_write(c, mem)):
            raise ValueError("no direct write between cores %d and %d" % (mem, c))
    return mem, fwd, back


def rank_program(g, core, T, topo):
    if T.rank_of(core) is None:
        return
    sem = T.sem
    mem, fwd, back = _roles(T, topo)
    KW = KB * P

    if core == back:
        m = topo.mask(core, mem)
        rid, pid, _ = topo.addr(mem)
        g.sync.dma_start(T.qd[:], T.q[:]).then_inc(sem.lq, 16)
        g.wait_ge(sem.lq, 16)
        g.remote_dma(T.qb[:], T.qd[:], remote_sem=sem.aq, local_sem=sem.sq, pid=pid, routing_id=rid,
                     dma_engine_mask=m)
        g.sync.wait_ge(sem.ay, _engines(topo.mask(mem, core)))
        g.sync.dma_start(T.y[:], T.yd[:]).then_inc(sem.st, 16)
        g.sync.wait_ge(sem.st, 16)
        g.wait_ge(sem.sq, _engines(m))
        return

    g.vector.memset(T.zero[:], 0.0).then_inc(sem.z, 1)
    g.vector.wait_ge(sem.z, 1)

    if core != mem:
        n = _engines(topo.mask(mem, core))
        g.sync.dma_start(T.qs[:], T.q[:]).then_inc(sem.lq, 16)
        _attend(g, T, 0, T.qs, T.s0, T.yo0, [("lq", 16), ("ak", n)], [("av", n)])
        g.sync.wait_ge(sem.c0, H)
        g.sync.dma_start(T.y[:], T.yo0[:]).then_inc(sem.st, 16)
        g.sync.wait_ge(sem.st, 16)
        return

    g.sync.dma_start(T.kv[:, 0:KW], T.k[:]).then_inc(sem.lk, 16)
    g.sync.dma_start(T.kv[:, KW:2 * KW], T.v[:]).then_inc(sem.lv, 16)
    g.sync.dma_start(T.qs[:], T.q[:]).then_inc(sem.lq, 16)

    mk = topo.mask(core, fwd[0])
    for c in fwd:
        mk &= topo.mask(core, c)
    ids = [DstId(rid=topo.addr(c)[0], pnc=topo.addr(c)[1]) for c in fwd]
    for lo, loaded, arrived in ((0, sem.lk, sem.ak), (KW, sem.lv, sem.av)):
        g.wait_ge(loaded, 16)
        g.remote_dma_fused([RemoteDMATransfer(
            dst_ids=ids, dma_engine_mask=mk, remote_sem=arrived, srcs=[T.kv[:, lo:lo + KW]],
            dsts=[T.kv[:, lo:lo + KW] for c in fwd], alu_op=0)], local_sem=sem.skv)

    _attend(g, T, 0, T.qs, T.s0, T.yo0, [("lk", 16), ("lq", 16)], [("lv", 16)])
    _attend(g, T, 1, T.qb, T.s1, T.yo1, [("aq", _engines(topo.mask(back, core)))], [("c0", H)])

    mb = topo.mask(core, back)
    rid, pid, _ = topo.addr(back)
    g.wait_ge(sem.c1, H)
    g.remote_dma(T.yd[:], T.yo1[:], remote_sem=sem.ay, local_sem=sem.sy, pid=pid, routing_id=rid,
                 dma_engine_mask=mb)

    g.sync.wait_ge(sem.c0, H)
    g.sync.wait_ge(sem.skv, 2 * _engines(mk))
    g.sync.dma_start(T.y[:], T.yo0[:]).then_inc(sem.st, 16)
    g.sync.wait_ge(sem.st, 16)
    g.wait_ge(sem.sy, _engines(mb))
